import numpy as np
import ml_dtypes


def mxq(x, axis, fmt="e4m3"):
    dtype, down = {"e4m3": (ml_dtypes.float8_e4m3fn, 7), "e5m2": (ml_dtypes.float8_e5m2, 14)}[fmt]
    v = np.moveaxis(np.asarray(x, np.float32).astype(ml_dtypes.bfloat16).astype(np.float64), axis, -1)
    blocks = v.reshape(v.shape[:-1] + (-1, 32))
    amax = np.abs(blocks).max(-1, keepdims=True)
    byte = np.maximum(np.where(amax > 0, np.frexp(amax)[1] - 1 + 127, 0) - down, 1)
    scale = np.exp2(byte - 127.0)
    codes = (blocks / scale).astype(np.float32).astype(dtype).astype(np.float64)
    return np.moveaxis((codes * scale).reshape(v.shape), -1, axis)


WIDE = False


def mx_kscale(k):
    if not WIDE:
        return np.ones(k)
    levels = np.array([10, -10, 5, -5, 0])
    if k % 512:
        return np.exp2(np.random.permutation(np.resize(levels, k // 32))).repeat(32)
    a = np.empty((k // 512, 16))
    for p in range(k // 512):
        a[p, :8] = np.random.permutation(np.resize(levels, 8))
        for g in range(8):
            far = levels[np.abs(levels - a[p, g]) >= 10]
            a[p, g + 8] = far[np.random.randint(len(far))]
    return np.exp2(a.ravel()).repeat(32)


def f64(x):
    return np.asarray(x).astype(np.float64)


def striped(idx):
    return np.tile(idx.reshape(-1, 16).T, (8, 1)).astype(np.uint16)


def unstriped(offs):
    return offs[:16].T.reshape(-1).astype(np.int64)


def striped8(idx):
    return np.concatenate([x.reshape(-1, 16).T for x in idx]).astype(np.uint16)


def runs(offs, k):
    lists = np.stack([offs[16 * r : 16 * r + 16].T.reshape(-1) for r in range(8)]).astype(np.int64)
    return lists[np.arange(k) % 512 // 64]


def pack_weight(w):
    k, n = w.shape
    w = f64(np.asarray(w, np.float32).astype(ml_dtypes.bfloat16)).reshape(k // 32, 32, n)
    amax = np.abs(w).max(1)
    byte = np.clip(np.where(amax > 0, np.frexp(amax)[1] - 1 + 127 - 7, 1), 1, 254)
    scaled = (w * np.exp2(127.0 - byte)[:, None, :]).reshape(k, n).astype(np.float32)
    words = np.ascontiguousarray(scaled.reshape(k // 512, 128, 4, n).transpose(0, 1, 3, 2)).astype(ml_dtypes.float8_e4m3fn).view(np.uint8)
    return words, np.ascontiguousarray(byte.astype(np.uint8).reshape(k // 512, 16, n))


def unpack_weight(words, scales):
    g, p, n, _ = words.shape
    vals = np.ascontiguousarray(words).view(ml_dtypes.float8_e4m3fn).astype(np.float64) * np.repeat(np.exp2(scales.astype(np.float64) - 127.0), 8, axis=1)[..., None]
    return vals.transpose(0, 1, 3, 2).reshape(g * 512, n)

def planes(y):
    n, m = y.shape
    v = y.astype(np.float32).astype(ml_dtypes.bfloat16).astype(np.float64).reshape(n // 32, 32, m)
    top = np.abs(v).max(1)
    byte = np.clip(np.where(top > 0, np.frexp(top)[1] - 1 + 127 - 7, 1), 1, 254)
    codes = (v * np.exp2(127.0 - byte)[:, None, :]).reshape(n, m).astype(np.float32).astype(ml_dtypes.float8_e4m3fn).view(np.uint8)
    words = codes.reshape(n // 512, 128, 4, m).transpose(0, 1, 3, 2)
    return np.ascontiguousarray(words), np.ascontiguousarray(byte.astype(np.uint8).reshape(n // 512, 16, m))


K, T, S, N, H, W = 512, 2048, 512, 512, 512, 256


def setup_inputs():
    n = np.random.standard_normal
    s = mx_kscale(K)[:, None]
    u = mx_kscale(S)
    packed_xT = pack_weight(n((K, T)) * s)
    packed_w1 = pack_weight(n((S, N)) / np.sqrt(S) / u[:, None])
    perm = np.stack([np.random.permutation(H) for _ in range(8)])
    return {
        "x_words": packed_xT[0],
        "x_scales": packed_xT[1],
        "wa": (n((K, H)) / np.sqrt(K) / s).astype(np.float32),
        "gt": (np.random.uniform(0.5, 1.5, (S, 1)) * u[:, None]).astype(np.float32),
        "w1_words": packed_w1[0],
        "w1_scales": packed_w1[1],
        "offs": striped(np.random.permutation(T)[:S]),
        "n1": striped8(perm[:, :W]),
        "n2": striped8(perm[:, W:]),
        "n3": striped8(np.stack([np.random.permutation(H) for _ in range(8)])),
        "n4": striped8(np.stack([np.random.permutation(H) for _ in range(8)])),
    }


def reference(x_words, x_scales, wa, gt, w1_words, w1_scales, offs, n1, n2, n3, n4):
    xq = unpack_weight(x_words, x_scales)[:, unstriped(offs)]
    y = xq.T @ mxq(f64(wa), 0, "e4m3")
    pa = y[np.arange(S)[:, None], runs(n1, S)]
    pb = y[np.arange(S)[:, None], runs(n2, S)]
    ra = np.maximum(pa, pb)
    ds = y.copy()
    ds[np.arange(S)[:, None], runs(n1, S)] = ra
    z = f64(gt) * ds
    h = unpack_weight(w1_words, w1_scales).T @ mxq(z, 0, "e4m3")
    st = h + h[np.arange(N)[:, None], runs(n3, N)]
    out_0 = st * (np.tanh(st[np.arange(N)[:, None], runs(n4, N)]))
    return (out_0,) + planes(out_0)

@@ -1,0 +1,232 @@
+from contextlib import ExitStack
+
+import concourse.mybir as mybir
+
+K, T, S, N, H, W = 512, 2048, 512, 512, 512, 256
+FLOPS = 2 * K * S * H + 2 * S * N * H
+
+F32 = mybir.dt.float32
+BF16 = mybir.dt.bfloat16
+I32 = mybir.dt.int32
+U32 = mybir.dt.uint32
+U16 = mybir.dt.uint16
+U8 = mybir.dt.uint8
+FP8X4 = mybir.dt.float8_e4m3fn_x4
+ALU = mybir.AluOpType
+ACT = mybir.ActivationFunctionType
+
+P = 128
+PACK = 4
+HALF = H // 2
+PER_COL = 16
+ROW_ORDER = (0, 2, 3, 1)
+WA_VECTOR_COLS = 176
+Z_VECTOR_COLS = 64
+OUT_CHUNKS = ((0, 256), (256, 384), (384, 512))
+
+
+def load_scale_rows(queue, plane, rows):
+    for q in range(4):
+        queue.dma_start(plane[32 * q : 32 * q + 4, :].bitcast(I32), rows[4 * q : 4 * q + 4, :].bitcast(I32))
+
+
+def interleave_views(grouped, planes, c0, c1):
+    dst = grouped[:, c0:c1, :].rearrange("p (c i) t -> p c t i", i=4)
+    src = planes[:, :, c0:c1].rearrange("p t (c i) -> p c t i", i=4)
+    return dst, src
+
+
+def tile_picked_tokfillhopp_none_po_kernel(
+    tc, x_words, x_scales, wa, gt, w1_words, w1_scales, offs, n1, n2, n3, n4, out_0, out_1, out_2
+):
+    nc = tc.nc
+    with ExitStack() as ctx:
+        keep = ctx.enter_context(tc.tile_pool(name="keep", bufs=1))
+        ring = ctx.enter_context(tc.tile_pool(name="ring", bufs=3))
+        psum = ctx.enter_context(tc.psum_pool(name="psum", bufs=8))
+
+        offs_t = keep.tile([P, S // PER_COL], U16, name="offs_t")
+        n1_t = keep.tile([P, W // PER_COL], U16, name="n1_t")
+        n2_t = keep.tile([P, W // PER_COL], U16, name="n2_t")
+        n3_t = keep.tile([P, H // PER_COL], U16, name="n3_t")
+        n4_t = keep.tile([P, H // PER_COL], U16, name="n4_t")
+        x_word_table = keep.tile([P, T], I32, name="x_word_table", align_bytes=64)
+        x_scale_table = keep.tile([P, T], U8, name="x_scale_table", align_bytes=64)
+        w1_word_raw = keep.tile([P, N], I32, name="w1_word_raw", align_bytes=64)
+        w1_scale_raw = keep.tile([P, N], U8, name="w1_scale_raw", align_bytes=64)
+        gt_t = keep.tile([P, PACK], F32, name="gt_t")
+        warm = keep.tile([P, 2], F32, name="warm")
+        wa_raw = [keep.tile([P, PACK, HALF], F32, name=f"wa_raw{a}") for a in range(2)]
+
+        nc.vector.memset(x_scale_table[:].bitcast(I32), 0)
+        nc.vector.memset(w1_scale_raw[:].bitcast(I32), 0)
+        nc.vector.memset(warm[:, 0:1], 0.0)
+
+        nc.sync.dma_start(offs_t[:], offs)
+        nc.sync.dma_start(x_word_table[:], x_words[0].rearrange("p c r -> p (c r)").bitcast(I32))
+        load_scale_rows(nc.sync, x_scale_table, x_scales[0])
+        nc.sync.dma_start(n1_t[:], n1)
+        nc.sync.dma_start(n2_t[:], n2)
+        wa_rows = wa.rearrange("(p j) c -> p j c", j=PACK)
+        for a in range(2):
+            nc.sync.dma_start(wa_raw[a][:], wa_rows[:, :, a * HALF : (a + 1) * HALF])
+        nc.sync.dma_start(w1_word_raw[:], w1_words[0].rearrange("p c r -> p (c r)").bitcast(I32))
+        load_scale_rows(nc.sync, w1_scale_raw, w1_scales[0])
+        nc.sync.dma_start(gt_t[:], gt.rearrange("(p t) o -> p (t o)", t=PACK))
+        nc.sync.dma_start(n3_t[:], n3)
+        nc.sync.dma_start(n4_t[:], n4)
+
+        nc.scalar.activation(warm[:, 1:2], warm[:, 0:1], ACT.Tanh)
+
+        x_scale_picked = keep.tile([P, S], U8, name="x_scale_picked", align_bytes=64)
+        x_scale_dealt = keep.tile([P, S], U8, name="x_scale_dealt", align_bytes=64)
+        x_word_dealt = keep.tile([P, S], U32, name="x_word_dealt", align_bytes=64)
+        nc.vector.tensor_copy(x_scale_picked[:], x_scale_table[:].indirect(offs_t[:]))
+        nc.vector.tensor_copy(
+            x_word_dealt[:].rearrange("p (t m) -> p m t", t=PACK), x_word_table[:].bitcast(U32).indirect(offs_t[:])
+        )
+        nc.vector.tensor_copy(
+            x_scale_dealt[:].rearrange("p (t m) -> p m t", t=PACK),
+            x_scale_picked[:].rearrange("p (m t) -> p m t", t=PACK),
+        )
+
+        wa_words, wa_scales = [], []
+        for a in range(2):
+            grouped = keep.tile([P, HALF, PACK], BF16, name=f"wa_grouped{a}", align_bytes=64)
+            words = keep.tile([P, HALF], U32, name=f"wa_words{a}", align_bytes=64)
+            scales = keep.tile([P, HALF], U8, name=f"wa_scales{a}", align_bytes=64)
+            split = WA_VECTOR_COLS if a == 1 else 0
+            if split:
+                nc.vector.tensor_copy(*interleave_views(grouped, wa_raw[a], 0, split))
+            nc.scalar.copy(*interleave_views(grouped, wa_raw[a], split, HALF))
+            nc.vector.quantize_mx(words[:].bitcast(FP8X4), scales[:], grouped[:].rearrange("p c t -> p (c t)"))
+            wa_words.append(words)
+            wa_scales.append(scales)
+
+        def product(lhs_words, lhs_scales, t, rhs_words, rhs_scales):
+            cols = slice(t * P, (t + 1) * P)
+            acc = psum.tile([P, HALF], F32, name="acc")
+            nc.tensor.matmul_mx(
+                acc[:],
+                lhsT=lhs_words[:, cols].bitcast(FP8X4),
+                lhsT_scale=lhs_scales[:, cols],
+                rhs=rhs_words[:].bitcast(FP8X4),
+                rhs_scale=rhs_scales[:],
+                start=True,
+                stop=True,
+            )
+            return acc
+
+        y_acc = {}
+        for a in range(2):
+            for t in ROW_ORDER:
+                y_acc[t, a] = product(x_word_dealt, x_scale_dealt, t, wa_words[a], wa_scales[a])
+
+        w1_word_dealt = keep.tile([P, N], I32, name="w1_word_dealt", align_bytes=64)
+        w1_scale_dealt = keep.tile([P, N], U8, name="w1_scale_dealt", align_bytes=64)
+
+        z_grouped = [keep.tile([P, HALF, PACK], BF16, name=f"z_grouped{a}", align_bytes=64) for a in range(2)]
+        for dealt, raw in ((w1_word_dealt, w1_word_raw), (w1_scale_dealt, w1_scale_raw)):
+            nc.vector.tensor_copy(
+                dealt[:].rearrange("p (t m) -> p m t", t=PACK), raw[:].rearrange("p (m t) -> p m t", t=PACK)
+            )
+        y_rows = {}
+
+        def fetch_y(t):
+            y_rows[t] = ring.tile([P, H], F32, name="y")
+            for a in range(2):
+                nc.scalar.copy(y_rows[t][:, a * HALF : (a + 1) * HALF], y_acc[t, a][:])
+
+        for t in ROW_ORDER[:-1]:
+            fetch_y(t)
+        for t in ROW_ORDER:
+            y = y_rows[t]
+            pa = ring.tile([P, W], F32, name="pa")
+            pb = ring.tile([P, W], F32, name="pb")
+            ra = ring.tile([P, W], F32, name="ra")
+            nc.vector.tensor_copy(pa[:], y[:].indirect(n1_t[:]))
+            nc.vector.tensor_copy(pb[:], y[:].indirect(n2_t[:]))
+            nc.vector.tensor_tensor(ra[:], pa[:], pb[:], ALU.max)
+            nc.vector.tensor_copy(y[:].indirect(n1_t[:]), ra[:])
+            gate = gt_t[:, t : t + 1]
+            on_vector = HALF + Z_VECTOR_COLS if t == ROW_ORDER[-1] else 0
+            for a in range(2):
+                split = min(max(on_vector - a * HALF, 0), HALF)
+                if split > 0:
+                    nc.vector.tensor_scalar(
+                        z_grouped[a][:, 0:split, t], y[:, a * HALF : a * HALF + split], gate, None, ALU.mult
+                    )
+                if split < HALF:
+                    nc.scalar.activation(
+                        z_grouped[a][:, split:HALF, t], y[:, a * HALF + split : (a + 1) * HALF], ACT.Copy, scale=gate
+                    )
+            if t == ROW_ORDER[0]:
+                fetch_y(ROW_ORDER[-1])
+
+        z_words, z_scales = [], []
+        for a in range(2):
+            words = keep.tile([P, HALF], U32, name=f"z_words{a}", align_bytes=64)
+            scales = keep.tile([P, HALF], U8, name=f"z_scales{a}", align_bytes=64)
+            nc.vector.quantize_mx(words[:].bitcast(FP8X4), scales[:], z_grouped[a][:].rearrange("p c t -> p (c t)"))
+            z_words.append(words)
+            z_scales.append(scales)
+
+        out_parts = [keep.tile([P, PACK, c1 - c0], F32, name=f"out_part{c0}") for c0, c1 in OUT_CHUNKS]
+        st, th = [], []
+
+        def gated(t, chunk):
+            c0, c1 = OUT_CHUNKS[chunk]
+            nc.vector.tensor_tensor(
+                out_parts[chunk][:, t, :],
+                th[t][:].indirect(n4_t[:, c0 // PER_COL : c1 // PER_COL]),
+                st[t][:, c0:c1],
+                ALU.mult,
+            )
+
+        for t in range(PACK):
+            h_window = keep.tile([P, H], F32, name=f"h_window{t}")
+            h_plain = keep.tile([P, H], F32, name=f"h_plain{t}")
+            st.append(keep.tile([P, H], F32, name=f"st{t}"))
+            th.append(keep.tile([P, H], F32, name=f"th{t}"))
+            accs = [product(w1_word_dealt, w1_scale_dealt, t, z_words[a], z_scales[a]) for a in range(2)]
+            for a in range(2):
+                nc.scalar.copy(h_window[:, a * HALF : (a + 1) * HALF], accs[a][:])
+            for a in range(2):
+                cols = slice(a * HALF, (a + 1) * HALF)
+                if t == 0 and a == 0:
+                    nc.vector.tensor_copy(h_plain[:, cols], accs[a][:])
+                else:
+                    nc.scalar.copy(h_plain[:, cols], accs[a][:])
+            for a in range(2):
+                cols = slice(a * HALF, (a + 1) * HALF)
+                offsets = n3_t[:, a * HALF // PER_COL : (a + 1) * HALF // PER_COL]
+                nc.vector.tensor_tensor(st[t][:, cols], h_window[:].indirect(offsets), h_plain[:, cols], ALU.add)
+            if t > 0:
+                nc.scalar.activation(th[t - 1][:], st[t - 1][:], ACT.Tanh)
+                gated(t - 1, 0)
+        nc.scalar.activation(th[PACK - 1][:], st[PACK - 1][:], ACT.Tanh)
+        gated(PACK - 1, 0)
+
+        out_scales = keep.tile([P, H], U8, name="out_scales", align_bytes=64)
+        out_rows = out_0.rearrange("(p t) c -> p t c", t=PACK)
+        out_words_dram = out_1[0].rearrange("p c r -> p (c r)").bitcast(I32)
+        last = len(OUT_CHUNKS) - 1
+        for chunk, (c0, c1) in enumerate(OUT_CHUNKS):
+            if chunk < last:
+                for t in range(PACK):
+                    gated(t, chunk + 1)
+            width = c1 - c0
+            nc.sync.dma_start(out_rows[:, :, c0:c1], out_parts[chunk][:])
+            grouped = keep.tile([P, width, PACK], BF16, name=f"out_grouped{c0}", align_bytes=64)
+            words = keep.tile([P, width], I32, name=f"out_words{c0}", align_bytes=64)
+            if chunk < last:
+                nc.scalar.copy(*interleave_views(grouped, out_parts[chunk], 0, width))
+            else:
+                nc.vector.tensor_copy(*interleave_views(grouped, out_parts[chunk], 0, width))
+            nc.vector.quantize_mx(
+                words[:].bitcast(FP8X4), out_scales[:, c0:c1], grouped[:].rearrange("p c t -> p (c t)")
+            )
+            nc.sync.dma_start(out_words_dram[:, c0:c1], words[:])
+        for q in range(4):
+            queue = nc.scalar if q % 2 else nc.sync
+            queue.dma_start(out_2[0][4 * q : 4 * q + 4, :].bitcast(I32), out_scales[32 * q : 32 * q + 4, :].bitcast(I32))

@@ -20,9 +20,12 @@ PACK = 4
 HALF = H // 2
 PER_COL = 16
 ROW_ORDER = (0, 2, 3, 1)
-WA_VECTOR_COLS = 176
-Z_VECTOR_COLS = 64
-OUT_CHUNKS = ((0, 256), (256, 384), (384, 512))
+WA_LOADS = ((0, 384), (384, 512))
+WA_STEPS = ((0, 0, 256), (0, 256, 384), (1, 384, 512))
+SCALE_ROWS = 16
+SCALE_ROW0 = 16
+Z_VECTOR_COLS = 80
+OUT_CHUNKS = ((0, 256), (256, 512))
 
 
 def load_scale_rows(queue, plane, rows):
@@ -30,9 +33,9 @@ def load_scale_rows(queue, plane, rows):
         queue.dma_start(plane[32 * q : 32 * q + 4, :].bitcast(I32), rows[4 * q : 4 * q + 4, :].bitcast(I32))
 
 
-def interleave_views(grouped, planes, c0, c1):
-    dst = grouped[:, c0:c1, :].rearrange("p (c i) t -> p c t i", i=4)
-    src = planes[:, :, c0:c1].rearrange("p t (c i) -> p c t i", i=4)
+def interleave_views(grouped, planes):
+    dst = grouped.rearrange("p (c i) t -> p c t i", i=4)
+    src = planes.rearrange("p t (c i) -> p c t i", i=4)
     return dst, src
 
 
@@ -50,104 +53,119 @@ def tile_picked_tokfillhopp_none_po_kernel(
         n2_t = keep.tile([P, W // PER_COL], U16, name="n2_t")
         n3_t = keep.tile([P, H // PER_COL], U16, name="n3_t")
         n4_t = keep.tile([P, H // PER_COL], U16, name="n4_t")
-        x_word_table = keep.tile([P, T], I32, name="x_word_table", align_bytes=64)
+        x_word_table = keep.tile([P, T], I32, name="x_word_table", tag="x_words", align_bytes=64)
         x_scale_table = keep.tile([P, T], U8, name="x_scale_table", align_bytes=64)
-        w1_word_raw = keep.tile([P, N], I32, name="w1_word_raw", align_bytes=64)
+        x_scale_plane = keep.tile([P, S], U8, name="x_scale_plane", align_bytes=64)
         w1_scale_raw = keep.tile([P, N], U8, name="w1_scale_raw", align_bytes=64)
         gt_t = keep.tile([P, PACK], F32, name="gt_t")
         warm = keep.tile([P, 2], F32, name="warm")
-        wa_raw = [keep.tile([P, PACK, HALF], F32, name=f"wa_raw{a}") for a in range(2)]
+        wa_raw = [
+            keep.tile([P, PACK, c1 - c0], F32, name=f"wa_raw{c0}", tag=f"staged{c0}", align_bytes=64)
+            for c0, c1 in WA_LOADS
+        ]
 
-        nc.vector.memset(x_scale_table[:].bitcast(I32), 0)
-        nc.vector.memset(w1_scale_raw[:].bitcast(I32), 0)
         nc.vector.memset(warm[:, 0:1], 0.0)
+        for p0, p1 in ((0, SCALE_ROW0), (SCALE_ROW0 + SCALE_ROWS, 64), (64, P)):
+            nc.vector.memset(x_scale_table[p0:p1, :].bitcast(I32), 0)
+        nc.vector.memset(x_scale_plane[:].bitcast(I32), 0)
+        nc.gpsimd.memset(w1_scale_raw[:].bitcast(I32), 0)
 
-        nc.sync.dma_start(offs_t[:], offs)
-        nc.sync.dma_start(x_word_table[:], x_words[0].rearrange("p c r -> p (c r)").bitcast(I32))
-        load_scale_rows(nc.sync, x_scale_table, x_scales[0])
-        nc.sync.dma_start(n1_t[:], n1)
-        nc.sync.dma_start(n2_t[:], n2)
         wa_rows = wa.rearrange("(p j) c -> p j c", j=PACK)
-        for a in range(2):
-            nc.sync.dma_start(wa_raw[a][:], wa_rows[:, :, a * HALF : (a + 1) * HALF])
-        nc.sync.dma_start(w1_word_raw[:], w1_words[0].rearrange("p c r -> p (c r)").bitcast(I32))
-        load_scale_rows(nc.sync, w1_scale_raw, w1_scales[0])
+        nc.sync.dma_start(offs_t[:], offs)
+        nc.sync.dma_start(
+            x_scale_table[SCALE_ROW0 : SCALE_ROW0 + SCALE_ROWS, :].bitcast(I32), x_scales[0].bitcast(I32)
+        )
+        nc.sync.dma_start(wa_raw[0][:], wa_rows[:, :, WA_LOADS[0][0] : WA_LOADS[0][1]])
+        for tile, index in ((n1_t, n1), (n2_t, n2), (n3_t, n3), (n4_t, n4)):
+            nc.sync.dma_start(tile[:], index)
+        nc.sync.dma_start(x_word_table[:], x_words[0].rearrange("p c r -> p (c r)").bitcast(I32))
+        nc.sync.dma_start(wa_raw[1][:], wa_rows[:, :, WA_LOADS[1][0] : WA_LOADS[1][1]])
         nc.sync.dma_start(gt_t[:], gt.rearrange("(p t) o -> p (t o)", t=PACK))
-        nc.sync.dma_start(n3_t[:], n3)
-        nc.sync.dma_start(n4_t[:], n4)
+        load_scale_rows(nc.gpsimd, w1_scale_raw, w1_scales[0])
 
         nc.scalar.activation(warm[:, 1:2], warm[:, 0:1], ACT.Tanh)
 
         x_scale_picked = keep.tile([P, S], U8, name="x_scale_picked", align_bytes=64)
-        x_scale_dealt = keep.tile([P, S], U8, name="x_scale_dealt", align_bytes=64)
+        x_scale_rows = keep.tile([P, S], U8, name="x_scale_rows", align_bytes=64)
         x_word_dealt = keep.tile([P, S], U32, name="x_word_dealt", align_bytes=64)
         nc.vector.tensor_copy(x_scale_picked[:], x_scale_table[:].indirect(offs_t[:]))
         nc.vector.tensor_copy(
+            x_scale_rows[:].rearrange("p (t m) -> p t m", t=PACK),
+            x_scale_picked[:].rearrange("p (m t) -> p t m", t=PACK),
+        )
+        load_scale_rows(nc.sync, x_scale_plane, x_scale_rows[SCALE_ROW0 : SCALE_ROW0 + SCALE_ROWS, :])
+        nc.vector.tensor_copy(
             x_word_dealt[:].rearrange("p (t m) -> p m t", t=PACK), x_word_table[:].bitcast(U32).indirect(offs_t[:])
         )
-        nc.vector.tensor_copy(
-            x_scale_dealt[:].rearrange("p (t m) -> p m t", t=PACK),
-            x_scale_picked[:].rearrange("p (m t) -> p m t", t=PACK),
-        )
 
-        wa_words, wa_scales = [], []
-        for a in range(2):
-            grouped = keep.tile([P, HALF, PACK], BF16, name=f"wa_grouped{a}", align_bytes=64)
-            words = keep.tile([P, HALF], U32, name=f"wa_words{a}", align_bytes=64)
-            scales = keep.tile([P, HALF], U8, name=f"wa_scales{a}", align_bytes=64)
-            split = WA_VECTOR_COLS if a == 1 else 0
-            if split:
-                nc.vector.tensor_copy(*interleave_views(grouped, wa_raw[a], 0, split))
-            nc.scalar.copy(*interleave_views(grouped, wa_raw[a], split, HALF))
-            nc.vector.quantize_mx(words[:].bitcast(FP8X4), scales[:], grouped[:].rearrange("p c t -> p (c t)"))
-            wa_words.append(words)
-            wa_scales.append(scales)
+        wa_words = keep.tile([P, H], U32, name="wa_words", align_bytes=64)
+        wa_scales = keep.tile([P, H], U8, name="wa_scales", align_bytes=64)
+        for load, c0, c1 in WA_STEPS:
+            grouped = keep.tile([P, c1 - c0, PACK], BF16, name=f"wa_grouped{c0}", align_bytes=64)
+            first = WA_LOADS[load][0]
+            nc.scalar.copy(*interleave_views(grouped[:], wa_raw[load][:, :, c0 - first : c1 - first]))
+            nc.vector.quantize_mx(
+                wa_words[:, c0:c1].bitcast(FP8X4), wa_scales[:, c0:c1], grouped[:].rearrange("p c t -> p (c t)")
+            )
+
+        w1_word_raw = keep.tile([P, N], I32, name="w1_word_raw", tag="staged0", align_bytes=64)
+        nc.sync.dma_start(w1_word_raw[:], w1_words[0].rearrange("p c r -> p (c r)").bitcast(I32))
 
         def product(lhs_words, lhs_scales, t, rhs_words, rhs_scales):
             cols = slice(t * P, (t + 1) * P)
-            acc = psum.tile([P, HALF], F32, name="acc")
+            acc = psum.tile([P, rhs_words.shape[1]], F32, name="acc")
             nc.tensor.matmul_mx(
                 acc[:],
                 lhsT=lhs_words[:, cols].bitcast(FP8X4),
                 lhsT_scale=lhs_scales[:, cols],
-                rhs=rhs_words[:].bitcast(FP8X4),
-                rhs_scale=rhs_scales[:],
+                rhs=rhs_words.bitcast(FP8X4),
+                rhs_scale=rhs_scales,
                 start=True,
                 stop=True,
             )
             return acc
 
         y_acc = {}
-        for a in range(2):
-            for t in ROW_ORDER:
-                y_acc[t, a] = product(x_word_dealt, x_scale_dealt, t, wa_words[a], wa_scales[a])
+        for t in ROW_ORDER:
+            for a in range(2):
+                cols = slice(a * HALF, (a + 1) * HALF)
+                y_acc[t, a] = product(x_word_dealt, x_scale_plane, t, wa_words[:, cols], wa_scales[:, cols])
 
         w1_word_dealt = keep.tile([P, N], I32, name="w1_word_dealt", align_bytes=64)
-        w1_scale_dealt = keep.tile([P, N], U8, name="w1_scale_dealt", align_bytes=64)
+        w1_scale_dealt = keep.tile([P, N], U8, name="w1_scale_dealt", tag="x_words", align_bytes=64)
 
         z_grouped = [keep.tile([P, HALF, PACK], BF16, name=f"z_grouped{a}", align_bytes=64) for a in range(2)]
-        for dealt, raw in ((w1_word_dealt, w1_word_raw), (w1_scale_dealt, w1_scale_raw)):
-            nc.vector.tensor_copy(
-                dealt[:].rearrange("p (t m) -> p m t", t=PACK), raw[:].rearrange("p (m t) -> p m t", t=PACK)
-            )
-        y_rows = {}
+        nc.vector.tensor_copy(
+            w1_word_dealt[:].rearrange("p (t m) -> p m t", t=PACK), w1_word_raw[:].rearrange("p (m t) -> p m t", t=PACK)
+        )
+        nc.vector.tensor_copy(
+            w1_scale_dealt[:].rearrange("p (t m) -> p t m", t=PACK),
+            w1_scale_raw[:].rearrange("p (m t) -> p t m", t=PACK),
+        )
+        y_rows, pa, rise = {}, {}, {}
 
         def fetch_y(t):
-            y_rows[t] = ring.tile([P, H], F32, name="y")
+            y_rows[t] = ring.tile([P, H], F32, name="y", tag="y", bufs=PACK)
             for a in range(2):
                 nc.scalar.copy(y_rows[t][:, a * HALF : (a + 1) * HALF], y_acc[t, a][:])
 
-        for t in ROW_ORDER[:-1]:
-            fetch_y(t)
-        for t in ROW_ORDER:
+        def compare(t):
+            pa[t] = keep.tile([P, W], F32, name=f"pa{t}")
+            gap = keep.tile([P, W], F32, name=f"gap{t}")
+            nc.vector.tensor_copy(pa[t][:], y_rows[t][:].indirect(n1_t[:]))
+            nc.vector.tensor_tensor(gap[:], y_rows[t][:].indirect(n2_t[:]), pa[t][:], ALU.subtract)
+            if t == ROW_ORDER[-1]:
+                weigh(ROW_ORDER[0])
+                rise[t] = ring.tile([P, W], F32, name="rise_last", tag="y", bufs=PACK)
+            else:
+                rise[t] = keep.tile([P, W], F32, name=f"rise{t}")
+            nc.scalar.activation(rise[t][:], gap[:], ACT.Relu)
+
+        def fill(t):
+            nc.vector.tensor_tensor(y_rows[t][:].indirect(n1_t[:]), pa[t][:], rise[t][:], ALU.add)
+
+        def weigh(t):
             y = y_rows[t]
-            pa = ring.tile([P, W], F32, name="pa")
-            pb = ring.tile([P, W], F32, name="pb")
-            ra = ring.tile([P, W], F32, name="ra")
-            nc.vector.tensor_copy(pa[:], y[:].indirect(n1_t[:]))
-            nc.vector.tensor_copy(pb[:], y[:].indirect(n2_t[:]))
-            nc.vector.tensor_tensor(ra[:], pa[:], pb[:], ALU.max)
-            nc.vector.tensor_copy(y[:].indirect(n1_t[:]), ra[:])
             gate = gt_t[:, t : t + 1]
             on_vector = HALF + Z_VECTOR_COLS if t == ROW_ORDER[-1] else 0
             for a in range(2):
@@ -160,18 +178,27 @@ def tile_picked_tokfillhopp_none_po_kernel(
                     nc.scalar.activation(
                         z_grouped[a][:, split:HALF, t], y[:, a * HALF + split : (a + 1) * HALF], ACT.Copy, scale=gate
                     )
-            if t == ROW_ORDER[0]:
-                fetch_y(ROW_ORDER[-1])
 
-        z_words, z_scales = [], []
+        for t in ROW_ORDER:
+            fetch_y(t)
+        for t in ROW_ORDER[:-1]:
+            compare(t)
+        fill(ROW_ORDER[0])
+        compare(ROW_ORDER[-1])
+        for t in ROW_ORDER[1:]:
+            fill(t)
+            weigh(t)
+
+        z_words = keep.tile([P, H], U32, name="z_words", align_bytes=64)
+        z_scales = keep.tile([P, H], U8, name="z_scales", align_bytes=64)
         for a in range(2):
-            words = keep.tile([P, HALF], U32, name=f"z_words{a}", align_bytes=64)
-            scales = keep.tile([P, HALF], U8, name=f"z_scales{a}", align_bytes=64)
-            nc.vector.quantize_mx(words[:].bitcast(FP8X4), scales[:], z_grouped[a][:].rearrange("p c t -> p (c t)"))
-            z_words.append(words)
-            z_scales.append(scales)
+            cols = slice(a * HALF, (a + 1) * HALF)
+            nc.vector.quantize_mx(
+                z_words[:, cols].bitcast(FP8X4), z_scales[:, cols], z_grouped[a][:].rearrange("p c t -> p (c t)")
+            )
 
         out_parts = [keep.tile([P, PACK, c1 - c0], F32, name=f"out_part{c0}") for c0, c1 in OUT_CHUNKS]
+        out_rows = out_0.rearrange("(p t) c -> p t c", t=PACK)
         st, th = [], []
 
         def gated(t, chunk):
@@ -182,21 +209,24 @@ def tile_picked_tokfillhopp_none_po_kernel(
                 st[t][:, c0:c1],
                 ALU.mult,
             )
+            if t >= PACK - 2:
+                rows = slice(0, PACK - 1) if t == PACK - 2 else slice(t, PACK)
+                nc.sync.dma_start(out_rows[:, rows, c0:c1], out_parts[chunk][:, rows, :])
 
         for t in range(PACK):
             h_window = keep.tile([P, H], F32, name=f"h_window{t}")
             h_plain = keep.tile([P, H], F32, name=f"h_plain{t}")
             st.append(keep.tile([P, H], F32, name=f"st{t}"))
             th.append(keep.tile([P, H], F32, name=f"th{t}"))
-            accs = [product(w1_word_dealt, w1_scale_dealt, t, z_words[a], z_scales[a]) for a in range(2)]
-            for a in range(2):
-                nc.scalar.copy(h_window[:, a * HALF : (a + 1) * HALF], accs[a][:])
-            for a in range(2):
-                cols = slice(a * HALF, (a + 1) * HALF)
-                if t == 0 and a == 0:
-                    nc.vector.tensor_copy(h_plain[:, cols], accs[a][:])
+            pieces = [slice(0, HALF), slice(HALF, H)] if t == 0 else [slice(0, H)]
+            accs = [product(w1_word_dealt, w1_scale_dealt, t, z_words[:, cols], z_scales[:, cols]) for cols in pieces]
+            for cols, acc in zip(pieces, accs):
+                nc.scalar.copy(h_window[:, cols], acc[:])
+            for cols, acc in zip(pieces, accs):
+                if cols.stop == HALF:
+                    nc.vector.tensor_copy(h_plain[:, cols], acc[:])
                 else:
-                    nc.scalar.copy(h_plain[:, cols], accs[a][:])
+                    nc.scalar.copy(h_plain[:, cols], acc[:])
             for a in range(2):
                 cols = slice(a * HALF, (a + 1) * HALF)
                 offsets = n3_t[:, a * HALF // PER_COL : (a + 1) * HALF // PER_COL]
@@ -208,7 +238,6 @@ def tile_picked_tokfillhopp_none_po_kernel(
         gated(PACK - 1, 0)
 
         out_scales = keep.tile([P, H], U8, name="out_scales", align_bytes=64)
-        out_rows = out_0.rearrange("(p t) c -> p t c", t=PACK)
         out_words_dram = out_1[0].rearrange("p c r -> p (c r)").bitcast(I32)
         last = len(OUT_CHUNKS) - 1
         for chunk, (c0, c1) in enumerate(OUT_CHUNKS):
@@ -216,13 +245,12 @@ def tile_picked_tokfillhopp_none_po_kernel(
                 for t in range(PACK):
                     gated(t, chunk + 1)
             width = c1 - c0
-            nc.sync.dma_start(out_rows[:, :, c0:c1], out_parts[chunk][:])
             grouped = keep.tile([P, width, PACK], BF16, name=f"out_grouped{c0}", align_bytes=64)
             words = keep.tile([P, width], I32, name=f"out_words{c0}", align_bytes=64)
             if chunk < last:
-                nc.scalar.copy(*interleave_views(grouped, out_parts[chunk], 0, width))
+                nc.scalar.copy(*interleave_views(grouped[:], out_parts[chunk][:]))
             else:
-                nc.vector.tensor_copy(*interleave_views(grouped, out_parts[chunk], 0, width))
+                nc.vector.tensor_copy(*interleave_views(grouped[:], out_parts[chunk][:]))
             nc.vector.quantize_mx(
                 words[:].bitcast(FP8X4), out_scales[:, c0:c1], grouped[:].rearrange("p c t -> p (c t)")
             )

@@ -24,7 +24,8 @@ WA_LOADS = ((0, 384), (384, 512))
 WA_STEPS = ((0, 0, 256), (0, 256, 384), (1, 384, 512))
 SCALE_ROWS = 16
 SCALE_ROW0 = 16
-Z_VECTOR_COLS = 80
+Z_PIECES = ((0, 256), (256, 384), (384, 512))
+Y_LATE_COLS = 64
 OUT_CHUNKS = ((0, 256), (256, 512))
 
 
@@ -111,8 +112,8 @@ def tile_picked_tokfillhopp_none_po_kernel(
         w1_word_raw = keep.tile([P, N], I32, name="w1_word_raw", tag="staged0", align_bytes=64)
         nc.sync.dma_start(w1_word_raw[:], w1_words[0].rearrange("p c r -> p (c r)").bitcast(I32))
 
-        def product(lhs_words, lhs_scales, t, rhs_words, rhs_scales):
-            cols = slice(t * P, (t + 1) * P)
+        def product(lhs_words, lhs_scales, slot, rhs_words, rhs_scales):
+            cols = slice(slot * P, (slot + 1) * P)
             acc = psum.tile([P, rhs_words.shape[1]], F32, name="acc")
             nc.tensor.matmul_mx(
                 acc[:],
@@ -125,76 +126,79 @@ def tile_picked_tokfillhopp_none_po_kernel(
             )
             return acc
 
+        first, second, third, last = ROW_ORDER
+        y_pieces = {
+            first: [(c0, c1) for load, c0, c1 in WA_STEPS],
+            second: [(0, HALF), (HALF, H)],
+            third: [(0, H)],
+            last: [(0, H)],
+        }
         y_acc = {}
         for t in ROW_ORDER:
-            for a in range(2):
-                cols = slice(a * HALF, (a + 1) * HALF)
-                y_acc[t, a] = product(x_word_dealt, x_scale_plane, t, wa_words[:, cols], wa_scales[:, cols])
+            for c0, c1 in y_pieces[t]:
+                y_acc[t, c0] = product(x_word_dealt, x_scale_plane, t, wa_words[:, c0:c1], wa_scales[:, c0:c1])
 
         w1_word_dealt = keep.tile([P, N], I32, name="w1_word_dealt", align_bytes=64)
         w1_scale_dealt = keep.tile([P, N], U8, name="w1_scale_dealt", tag="x_words", align_bytes=64)
-
-        z_grouped = [keep.tile([P, HALF, PACK], BF16, name=f"z_grouped{a}", align_bytes=64) for a in range(2)]
-        nc.vector.tensor_copy(
-            w1_word_dealt[:].rearrange("p (t m) -> p m t", t=PACK), w1_word_raw[:].rearrange("p (m t) -> p m t", t=PACK)
-        )
         nc.vector.tensor_copy(
             w1_scale_dealt[:].rearrange("p (t m) -> p t m", t=PACK),
             w1_scale_raw[:].rearrange("p (m t) -> p t m", t=PACK),
         )
-        y_rows, pa, rise = {}, {}, {}
+        nc.vector.tensor_copy(
+            w1_word_dealt[:].rearrange("p (t m) -> p m t", t=PACK), w1_word_raw[:].rearrange("p (m t) -> p m t", t=PACK)
+        )
 
-        def fetch_y(t):
-            y_rows[t] = ring.tile([P, H], F32, name="y", tag="y", bufs=PACK)
-            for a in range(2):
-                nc.scalar.copy(y_rows[t][:, a * HALF : (a + 1) * HALF], y_acc[t, a][:])
+        z_grouped = [
+            keep.tile([P, c1 - c0, PACK], BF16, name=f"z_grouped{c0}", align_bytes=64)
+            for c0, c1 in Z_PIECES
+        ]
+        y_rows = {t: ring.tile([P, H], F32, name=f"y{t}", tag="y", bufs=PACK) for t in ROW_ORDER}
+        for t in (first, second):
+            for c0, c1 in y_pieces[t]:
+                nc.scalar.copy(y_rows[t][:, c0:c1], y_acc[t, c0][:])
+        early = H - Y_LATE_COLS
+        nc.scalar.copy(y_rows[last][:, 0:early], y_acc[last, 0][:, 0:early])
+        nc.scalar.copy(y_rows[third][:], y_acc[third, 0][:])
+        nc.scalar.copy(y_rows[last][:, early:H], y_acc[last, 0][:, early:H])
 
-        def compare(t):
-            pa[t] = keep.tile([P, W], F32, name=f"pa{t}")
-            gap = keep.tile([P, W], F32, name=f"gap{t}")
-            nc.vector.tensor_copy(pa[t][:], y_rows[t][:].indirect(n1_t[:]))
-            nc.vector.tensor_tensor(gap[:], y_rows[t][:].indirect(n2_t[:]), pa[t][:], ALU.subtract)
-            if t == ROW_ORDER[-1]:
-                weigh(ROW_ORDER[0])
-                rise[t] = ring.tile([P, W], F32, name="rise_last", tag="y", bufs=PACK)
-            else:
-                rise[t] = keep.tile([P, W], F32, name=f"rise{t}")
-            nc.scalar.activation(rise[t][:], gap[:], ACT.Relu)
+        pa = {t: keep.tile([P, W], F32, name=f"pa{t}") for t in ROW_ORDER}
+        gap = {t: keep.tile([P, W], F32, name=f"gap{t}") for t in ROW_ORDER}
+        rise = {}
+
+        def rectify(t, tile):
+            rise[t] = tile
+            nc.scalar.activation(rise[t][:], gap[t][:], ACT.Relu)
 
         def fill(t):
             nc.vector.tensor_tensor(y_rows[t][:].indirect(n1_t[:]), pa[t][:], rise[t][:], ALU.add)
 
         def weigh(t):
-            y = y_rows[t]
             gate = gt_t[:, t : t + 1]
-            on_vector = HALF + Z_VECTOR_COLS if t == ROW_ORDER[-1] else 0
-            for a in range(2):
-                split = min(max(on_vector - a * HALF, 0), HALF)
-                if split > 0:
-                    nc.vector.tensor_scalar(
-                        z_grouped[a][:, 0:split, t], y[:, a * HALF : a * HALF + split], gate, None, ALU.mult
-                    )
-                if split < HALF:
-                    nc.scalar.activation(
-                        z_grouped[a][:, split:HALF, t], y[:, a * HALF + split : (a + 1) * HALF], ACT.Copy, scale=gate
-                    )
+            for piece, (c0, c1) in enumerate(Z_PIECES):
+                if t == last and c1 < H:
+                    nc.vector.tensor_scalar(z_grouped[piece][:, :, t], y_rows[t][:, c0:c1], gate, None, ALU.mult)
+                else:
+                    nc.scalar.activation(z_grouped[piece][:, :, t], y_rows[t][:, c0:c1], ACT.Copy, scale=gate)
 
-        for t in ROW_ORDER:
-            fetch_y(t)
-        for t in ROW_ORDER[:-1]:
-            compare(t)
-        fill(ROW_ORDER[0])
-        compare(ROW_ORDER[-1])
-        for t in ROW_ORDER[1:]:
+        for pair in ((first, second), (third, last)):
+            for t in pair:
+                nc.vector.tensor_copy(pa[t][:], y_rows[t][:].indirect(n1_t[:]))
+            for t in pair:
+                nc.vector.tensor_tensor(gap[t][:], y_rows[t][:].indirect(n2_t[:]), pa[t][:], ALU.subtract)
+        for t in (first, second, third):
+            rectify(t, keep.tile([P, W], F32, name=f"rise{t}"))
+        fill(first)
+        weigh(first)
+        rectify(last, ring.tile([P, W], F32, name="rise_last", tag="y", bufs=PACK))
+        for t in (second, third, last):
             fill(t)
             weigh(t)
 
         z_words = keep.tile([P, H], U32, name="z_words", align_bytes=64)
         z_scales = keep.tile([P, H], U8, name="z_scales", align_bytes=64)
-        for a in range(2):
-            cols = slice(a * HALF, (a + 1) * HALF)
+        for piece, (c0, c1) in enumerate(Z_PIECES):
             nc.vector.quantize_mx(
-                z_words[:, cols].bitcast(FP8X4), z_scales[:, cols], z_grouped[a][:].rearrange("p c t -> p (c t)")
+                z_words[:, c0:c1].bitcast(FP8X4), z_scales[:, c0:c1], z_grouped[piece][:].rearrange("p c t -> p (c t)")
             )
 
         out_parts = [keep.tile([P, PACK, c1 - c0], F32, name=f"out_part{c0}") for c0, c1 in OUT_CHUNKS]
@@ -218,12 +222,12 @@ def tile_picked_tokfillhopp_none_po_kernel(
             h_plain = keep.tile([P, H], F32, name=f"h_plain{t}")
             st.append(keep.tile([P, H], F32, name=f"st{t}"))
             th.append(keep.tile([P, H], F32, name=f"th{t}"))
-            pieces = [slice(0, HALF), slice(HALF, H)] if t == 0 else [slice(0, H)]
+            pieces = [slice(c0, c1) for c0, c1 in Z_PIECES] if t == 0 else [slice(0, H)]
             accs = [product(w1_word_dealt, w1_scale_dealt, t, z_words[:, cols], z_scales[:, cols]) for cols in pieces]
             for cols, acc in zip(pieces, accs):
                 nc.scalar.copy(h_window[:, cols], acc[:])
             for cols, acc in zip(pieces, accs):
-                if cols.stop == HALF:
+                if cols.stop < H:
                     nc.vector.tensor_copy(h_plain[:, cols], acc[:])
                 else:
                     nc.scalar.copy(h_plain[:, cols], acc[:])
@@ -239,15 +243,15 @@ def tile_picked_tokfillhopp_none_po_kernel(
 
         out_scales = keep.tile([P, H], U8, name="out_scales", align_bytes=64)
         out_words_dram = out_1[0].rearrange("p c r -> p (c r)").bitcast(I32)
-        last = len(OUT_CHUNKS) - 1
+        last_chunk = len(OUT_CHUNKS) - 1
         for chunk, (c0, c1) in enumerate(OUT_CHUNKS):
-            if chunk < last:
+            if chunk < last_chunk:
                 for t in range(PACK):
                     gated(t, chunk + 1)
             width = c1 - c0
             grouped = keep.tile([P, width, PACK], BF16, name=f"out_grouped{c0}", align_bytes=64)
             words = keep.tile([P, width], I32, name=f"out_words{c0}", align_bytes=64)
-            if chunk < last:
+            if chunk < last_chunk:
                 nc.scalar.copy(*interleave_views(grouped[:], out_parts[chunk][:]))
             else:
                 nc.vector.tensor_copy(*interleave_views(grouped[:], out_parts[chunk][:]))

@@ -59,32 +59,28 @@ def tile_picked_tokfillhopp_none_po_kernel(
         x_scale_plane = keep.tile([P, S], U8, name="x_scale_plane", align_bytes=64)
         w1_scale_raw = keep.tile([P, N], U8, name="w1_scale_raw", align_bytes=64)
         gt_t = keep.tile([P, PACK], F32, name="gt_t")
-        warm = keep.tile([P, 2], F32, name="warm")
         wa_raw = [
             keep.tile([P, PACK, c1 - c0], F32, name=f"wa_raw{c0}", tag=f"staged{c0}", align_bytes=64)
             for c0, c1 in WA_LOADS
         ]
 
-        nc.vector.memset(warm[:, 0:1], 0.0)
         for p0, p1 in ((0, SCALE_ROW0), (SCALE_ROW0 + SCALE_ROWS, 64), (64, P)):
             nc.vector.memset(x_scale_table[p0:p1, :].bitcast(I32), 0)
         nc.vector.memset(x_scale_plane[:].bitcast(I32), 0)
         nc.gpsimd.memset(w1_scale_raw[:].bitcast(I32), 0)
 
         wa_rows = wa.rearrange("(p j) c -> p j c", j=PACK)
+        nc.sync.dma_start(wa_raw[0][:], wa_rows[:, :, WA_LOADS[0][0] : WA_LOADS[0][1]])
         nc.sync.dma_start(offs_t[:], offs)
         nc.sync.dma_start(
             x_scale_table[SCALE_ROW0 : SCALE_ROW0 + SCALE_ROWS, :].bitcast(I32), x_scales[0].bitcast(I32)
         )
-        nc.sync.dma_start(wa_raw[0][:], wa_rows[:, :, WA_LOADS[0][0] : WA_LOADS[0][1]])
         for tile, index in ((n1_t, n1), (n2_t, n2), (n3_t, n3), (n4_t, n4)):
             nc.sync.dma_start(tile[:], index)
         nc.sync.dma_start(x_word_table[:], x_words[0].rearrange("p c r -> p (c r)").bitcast(I32))
         nc.sync.dma_start(wa_raw[1][:], wa_rows[:, :, WA_LOADS[1][0] : WA_LOADS[1][1]])
         nc.sync.dma_start(gt_t[:], gt.rearrange("(p t) o -> p (t o)", t=PACK))
         load_scale_rows(nc.gpsimd, w1_scale_raw, w1_scales[0])
-
-        nc.scalar.activation(warm[:, 1:2], warm[:, 0:1], ACT.Tanh)
 
         x_scale_picked = keep.tile([P, S], U8, name="x_scale_picked", align_bytes=64)
         x_scale_rows = keep.tile([P, S], U8, name="x_scale_rows", align_bytes=64)

@@ -17,27 +17,41 @@ ACT = mybir.ActivationFunctionType
 
 P = 128
 PACK = 4
+QUADRANTS = 4
 HALF = H // 2
 PER_COL = 16
+
+SCALE_ROWS = slice(16, 32)
+OTHER_ROWS = (slice(0, 16), slice(32, 64), slice(64, P))
+
 ROW_ORDER = (0, 2, 3, 1)
+
 WA_LOADS = ((0, 384), (384, 512))
 WA_STEPS = ((0, 0, 256), (0, 256, 384), (1, 384, 512))
-SCALE_ROWS = 16
-SCALE_ROW0 = 16
 Z_PIECES = ((0, 256), (256, 384), (384, 512))
 Y_LATE_COLS = 64
 OUT_CHUNKS = ((0, 256), (256, 512))
 
 
-def load_scale_rows(queue, plane, rows):
-    for q in range(4):
-        queue.dma_start(plane[32 * q : 32 * q + 4, :].bitcast(I32), rows[4 * q : 4 * q + 4, :].bitcast(I32))
+def spread_scale_rows(nc, plane, rows):
+    for q in range(QUADRANTS):
+        nc.sync.dma_start(plane[32 * q : 32 * q + 4, :].bitcast(I32), rows[4 * q : 4 * q + 4, :].bitcast(I32))
 
 
-def interleave_views(grouped, planes):
+def deal_scale_bytes(nc, dealt, plain):
+    nc.vector.tensor_copy(
+        dealt[:].rearrange("p (t m) -> p t m", t=PACK), plain[:].rearrange("p (m t) -> p t m", t=PACK)
+    )
+
+
+def interleave_views(grouped, row_tiles):
     dst = grouped.rearrange("p (c i) t -> p c t i", i=4)
-    src = planes.rearrange("p t (c i) -> p c t i", i=4)
+    src = row_tiles.rearrange("p t (c i) -> p c t i", i=4)
     return dst, src
+
+
+def quantize(nc, words, scales, grouped):
+    nc.vector.quantize_mx(words.bitcast(FP8X4), scales, grouped[:].rearrange("p c t -> p (c t)"))
 
 
 def tile_picked_tokfillhopp_none_po_kernel(
@@ -46,7 +60,7 @@ def tile_picked_tokfillhopp_none_po_kernel(
     nc = tc.nc
     with ExitStack() as ctx:
         keep = ctx.enter_context(tc.tile_pool(name="keep", bufs=1))
-        ring = ctx.enter_context(tc.tile_pool(name="ring", bufs=3))
+        y_pool = ctx.enter_context(tc.tile_pool(name="y_pool", bufs=PACK))
         psum = ctx.enter_context(tc.psum_pool(name="psum", bufs=8))
 
         offs_t = keep.tile([P, S // PER_COL], U16, name="offs_t")
@@ -57,40 +71,37 @@ def tile_picked_tokfillhopp_none_po_kernel(
         x_word_table = keep.tile([P, T], I32, name="x_word_table", tag="x_words", align_bytes=64)
         x_scale_table = keep.tile([P, T], U8, name="x_scale_table", align_bytes=64)
         x_scale_plane = keep.tile([P, S], U8, name="x_scale_plane", align_bytes=64)
-        w1_scale_raw = keep.tile([P, N], U8, name="w1_scale_raw", align_bytes=64)
+        w1_scale_table = keep.tile([P, N], U8, name="w1_scale_table", align_bytes=64)
         gt_t = keep.tile([P, PACK], F32, name="gt_t")
         wa_raw = [
             keep.tile([P, PACK, c1 - c0], F32, name=f"wa_raw{c0}", tag=f"staged{c0}", align_bytes=64)
             for c0, c1 in WA_LOADS
         ]
 
-        for p0, p1 in ((0, SCALE_ROW0), (SCALE_ROW0 + SCALE_ROWS, 64), (64, P)):
-            nc.vector.memset(x_scale_table[p0:p1, :].bitcast(I32), 0)
+        for table in (x_scale_table, w1_scale_table):
+            for rows in OTHER_ROWS:
+                nc.vector.memset(table[rows, :].bitcast(I32), 0)
         nc.vector.memset(x_scale_plane[:].bitcast(I32), 0)
-        nc.gpsimd.memset(w1_scale_raw[:].bitcast(I32), 0)
 
         wa_rows = wa.rearrange("(p j) c -> p j c", j=PACK)
-        nc.sync.dma_start(wa_raw[0][:], wa_rows[:, :, WA_LOADS[0][0] : WA_LOADS[0][1]])
         nc.sync.dma_start(offs_t[:], offs)
-        nc.sync.dma_start(
-            x_scale_table[SCALE_ROW0 : SCALE_ROW0 + SCALE_ROWS, :].bitcast(I32), x_scales[0].bitcast(I32)
-        )
-        for tile, index in ((n1_t, n1), (n2_t, n2), (n3_t, n3), (n4_t, n4)):
-            nc.sync.dma_start(tile[:], index)
+        for table, scale_input in ((x_scale_table, x_scales), (w1_scale_table, w1_scales)):
+            nc.sync.dma_start(table[SCALE_ROWS, :].bitcast(I32), scale_input[0].bitcast(I32))
+        nc.sync.dma_start(wa_raw[0][:], wa_rows[:, :, WA_LOADS[0][0] : WA_LOADS[0][1]])
+        for list_tile, list_input in ((n1_t, n1), (n2_t, n2), (n3_t, n3), (n4_t, n4)):
+            nc.sync.dma_start(list_tile[:], list_input)
         nc.sync.dma_start(x_word_table[:], x_words[0].rearrange("p c r -> p (c r)").bitcast(I32))
         nc.sync.dma_start(wa_raw[1][:], wa_rows[:, :, WA_LOADS[1][0] : WA_LOADS[1][1]])
         nc.sync.dma_start(gt_t[:], gt.rearrange("(p t) o -> p (t o)", t=PACK))
-        load_scale_rows(nc.gpsimd, w1_scale_raw, w1_scales[0])
 
         x_scale_picked = keep.tile([P, S], U8, name="x_scale_picked", align_bytes=64)
-        x_scale_rows = keep.tile([P, S], U8, name="x_scale_rows", align_bytes=64)
+        x_scale_dealt = keep.tile([P, S], U8, name="x_scale_dealt", align_bytes=64)
         x_word_dealt = keep.tile([P, S], U32, name="x_word_dealt", align_bytes=64)
         nc.vector.tensor_copy(x_scale_picked[:], x_scale_table[:].indirect(offs_t[:]))
-        nc.vector.tensor_copy(
-            x_scale_rows[:].rearrange("p (t m) -> p t m", t=PACK),
-            x_scale_picked[:].rearrange("p (m t) -> p t m", t=PACK),
-        )
-        load_scale_rows(nc.sync, x_scale_plane, x_scale_rows[SCALE_ROW0 : SCALE_ROW0 + SCALE_ROWS, :])
+        deal_scale_bytes(nc, x_scale_dealt, x_scale_picked)
+        spread_scale_rows(nc, x_scale_plane, x_scale_dealt[SCALE_ROWS, :])
+        w1_scale_dealt = keep.tile([P, N], U8, name="w1_scale_dealt", align_bytes=64)
+        deal_scale_bytes(nc, w1_scale_dealt, w1_scale_table)
         nc.vector.tensor_copy(
             x_word_dealt[:].rearrange("p (t m) -> p m t", t=PACK), x_word_table[:].bitcast(U32).indirect(offs_t[:])
         )
@@ -98,23 +109,21 @@ def tile_picked_tokfillhopp_none_po_kernel(
         wa_words = keep.tile([P, H], U32, name="wa_words", align_bytes=64)
         wa_scales = keep.tile([P, H], U8, name="wa_scales", align_bytes=64)
         for load, c0, c1 in WA_STEPS:
-            grouped = keep.tile([P, c1 - c0, PACK], BF16, name=f"wa_grouped{c0}", align_bytes=64)
-            first = WA_LOADS[load][0]
-            nc.scalar.copy(*interleave_views(grouped[:], wa_raw[load][:, :, c0 - first : c1 - first]))
-            nc.vector.quantize_mx(
-                wa_words[:, c0:c1].bitcast(FP8X4), wa_scales[:, c0:c1], grouped[:].rearrange("p c t -> p (c t)")
-            )
+            wa_grouped = keep.tile([P, c1 - c0, PACK], BF16, name=f"wa_grouped{c0}", align_bytes=64)
+            load_start = WA_LOADS[load][0]
+            nc.scalar.copy(*interleave_views(wa_grouped[:], wa_raw[load][:, :, c0 - load_start : c1 - load_start]))
+            quantize(nc, wa_words[:, c0:c1], wa_scales[:, c0:c1], wa_grouped)
 
         w1_word_raw = keep.tile([P, N], I32, name="w1_word_raw", tag="staged0", align_bytes=64)
         nc.sync.dma_start(w1_word_raw[:], w1_words[0].rearrange("p c r -> p (c r)").bitcast(I32))
 
-        def product(lhs_words, lhs_scales, slot, rhs_words, rhs_scales):
-            cols = slice(slot * P, (slot + 1) * P)
+        def product(lhs_words, lhs_scales, t, rhs_words, rhs_scales):
+            dealt_cols = slice(t * P, (t + 1) * P)
             acc = psum.tile([P, rhs_words.shape[1]], F32, name="acc")
             nc.tensor.matmul_mx(
                 acc[:],
-                lhsT=lhs_words[:, cols].bitcast(FP8X4),
-                lhsT_scale=lhs_scales[:, cols],
+                lhsT=lhs_words[:, dealt_cols].bitcast(FP8X4),
+                lhsT_scale=lhs_scales[:, dealt_cols],
                 rhs=rhs_words.bitcast(FP8X4),
                 rhs_scale=rhs_scales,
                 start=True,
@@ -135,20 +144,17 @@ def tile_picked_tokfillhopp_none_po_kernel(
                 y_acc[t, c0] = product(x_word_dealt, x_scale_plane, t, wa_words[:, c0:c1], wa_scales[:, c0:c1])
 
         w1_word_dealt = keep.tile([P, N], I32, name="w1_word_dealt", align_bytes=64)
-        w1_scale_dealt = keep.tile([P, N], U8, name="w1_scale_dealt", tag="x_words", align_bytes=64)
-        nc.vector.tensor_copy(
-            w1_scale_dealt[:].rearrange("p (t m) -> p t m", t=PACK),
-            w1_scale_raw[:].rearrange("p (m t) -> p t m", t=PACK),
-        )
+        w1_scale_plane = keep.tile([P, N], U8, name="w1_scale_plane", tag="x_words", align_bytes=64)
+        nc.vector.memset(w1_scale_plane[:].bitcast(I32), 0)
+        spread_scale_rows(nc, w1_scale_plane, w1_scale_dealt[SCALE_ROWS, :])
         nc.vector.tensor_copy(
             w1_word_dealt[:].rearrange("p (t m) -> p m t", t=PACK), w1_word_raw[:].rearrange("p (m t) -> p m t", t=PACK)
         )
 
         z_grouped = [
-            keep.tile([P, c1 - c0, PACK], BF16, name=f"z_grouped{c0}", align_bytes=64)
-            for c0, c1 in Z_PIECES
+            keep.tile([P, c1 - c0, PACK], BF16, name=f"z_grouped{c0}", align_bytes=64) for c0, c1 in Z_PIECES
         ]
-        y_rows = {t: ring.tile([P, H], F32, name=f"y{t}", tag="y", bufs=PACK) for t in ROW_ORDER}
+        y_rows = {t: y_pool.tile([P, H], F32, name=f"y{t}", tag="y") for t in ROW_ORDER}
         for t in (first, second):
             for c0, c1 in y_pieces[t]:
                 nc.scalar.copy(y_rows[t][:, c0:c1], y_acc[t, c0][:])
@@ -158,12 +164,12 @@ def tile_picked_tokfillhopp_none_po_kernel(
         nc.scalar.copy(y_rows[last][:, early:H], y_acc[last, 0][:, early:H])
 
         pa = {t: keep.tile([P, W], F32, name=f"pa{t}") for t in ROW_ORDER}
-        gap = {t: keep.tile([P, W], F32, name=f"gap{t}") for t in ROW_ORDER}
+        pb_less_pa = {t: keep.tile([P, W], F32, name=f"pb_less_pa{t}") for t in ROW_ORDER}
         rise = {}
 
         def rectify(t, tile):
             rise[t] = tile
-            nc.scalar.activation(rise[t][:], gap[t][:], ACT.Relu)
+            nc.scalar.activation(rise[t][:], pb_less_pa[t][:], ACT.Relu)
 
         def fill(t):
             nc.vector.tensor_tensor(y_rows[t][:].indirect(n1_t[:]), pa[t][:], rise[t][:], ALU.add)
@@ -180,12 +186,12 @@ def tile_picked_tokfillhopp_none_po_kernel(
             for t in pair:
                 nc.vector.tensor_copy(pa[t][:], y_rows[t][:].indirect(n1_t[:]))
             for t in pair:
-                nc.vector.tensor_tensor(gap[t][:], y_rows[t][:].indirect(n2_t[:]), pa[t][:], ALU.subtract)
+                nc.vector.tensor_tensor(pb_less_pa[t][:], y_rows[t][:].indirect(n2_t[:]), pa[t][:], ALU.subtract)
         for t in (first, second, third):
             rectify(t, keep.tile([P, W], F32, name=f"rise{t}"))
         fill(first)
         weigh(first)
-        rectify(last, ring.tile([P, W], F32, name="rise_last", tag="y", bufs=PACK))
+        rectify(last, y_pool.tile([P, W], F32, name="rise_last", tag="y"))
         for t in (second, third, last):
             fill(t)
             weigh(t)
@@ -193,33 +199,31 @@ def tile_picked_tokfillhopp_none_po_kernel(
         z_words = keep.tile([P, H], U32, name="z_words", align_bytes=64)
         z_scales = keep.tile([P, H], U8, name="z_scales", align_bytes=64)
         for piece, (c0, c1) in enumerate(Z_PIECES):
-            nc.vector.quantize_mx(
-                z_words[:, c0:c1].bitcast(FP8X4), z_scales[:, c0:c1], z_grouped[piece][:].rearrange("p c t -> p (c t)")
-            )
+            quantize(nc, z_words[:, c0:c1], z_scales[:, c0:c1], z_grouped[piece])
 
         out_parts = [keep.tile([P, PACK, c1 - c0], F32, name=f"out_part{c0}") for c0, c1 in OUT_CHUNKS]
         out_rows = out_0.rearrange("(p t) c -> p t c", t=PACK)
-        st, th = [], []
+        st, tanh_st = [], []
 
         def gated(t, chunk):
             c0, c1 = OUT_CHUNKS[chunk]
             nc.vector.tensor_tensor(
                 out_parts[chunk][:, t, :],
-                th[t][:].indirect(n4_t[:, c0 // PER_COL : c1 // PER_COL]),
+                tanh_st[t][:].indirect(n4_t[:, c0 // PER_COL : c1 // PER_COL]),
                 st[t][:, c0:c1],
                 ALU.mult,
             )
             if t >= PACK - 2:
-                rows = slice(0, PACK - 1) if t == PACK - 2 else slice(t, PACK)
-                nc.sync.dma_start(out_rows[:, rows, c0:c1], out_parts[chunk][:, rows, :])
+                stored = slice(0, PACK - 1) if t == PACK - 2 else slice(t, PACK)
+                nc.sync.dma_start(out_rows[:, stored, c0:c1], out_parts[chunk][:, stored, :])
 
         for t in range(PACK):
             h_window = keep.tile([P, H], F32, name=f"h_window{t}")
             h_plain = keep.tile([P, H], F32, name=f"h_plain{t}")
             st.append(keep.tile([P, H], F32, name=f"st{t}"))
-            th.append(keep.tile([P, H], F32, name=f"th{t}"))
+            tanh_st.append(keep.tile([P, H], F32, name=f"tanh_st{t}"))
             pieces = [slice(c0, c1) for c0, c1 in Z_PIECES] if t == 0 else [slice(0, H)]
-            accs = [product(w1_word_dealt, w1_scale_dealt, t, z_words[:, cols], z_scales[:, cols]) for cols in pieces]
+            accs = [product(w1_word_dealt, w1_scale_plane, t, z_words[:, cols], z_scales[:, cols]) for cols in pieces]
             for cols, acc in zip(pieces, accs):
                 nc.scalar.copy(h_window[:, cols], acc[:])
             for cols, acc in zip(pieces, accs):
@@ -227,34 +231,28 @@ def tile_picked_tokfillhopp_none_po_kernel(
                     nc.vector.tensor_copy(h_plain[:, cols], acc[:])
                 else:
                     nc.scalar.copy(h_plain[:, cols], acc[:])
-            for a in range(2):
-                cols = slice(a * HALF, (a + 1) * HALF)
-                offsets = n3_t[:, a * HALF // PER_COL : (a + 1) * HALF // PER_COL]
-                nc.vector.tensor_tensor(st[t][:, cols], h_window[:].indirect(offsets), h_plain[:, cols], ALU.add)
+            for c0 in (0, HALF):
+                offsets = n3_t[:, c0 // PER_COL : (c0 + HALF) // PER_COL]
+                nc.vector.tensor_tensor(
+                    st[t][:, c0 : c0 + HALF], h_window[:].indirect(offsets), h_plain[:, c0 : c0 + HALF], ALU.add
+                )
             if t > 0:
-                nc.scalar.activation(th[t - 1][:], st[t - 1][:], ACT.Tanh)
+                nc.scalar.activation(tanh_st[t - 1][:], st[t - 1][:], ACT.Tanh)
                 gated(t - 1, 0)
-        nc.scalar.activation(th[PACK - 1][:], st[PACK - 1][:], ACT.Tanh)
+        nc.scalar.activation(tanh_st[PACK - 1][:], st[PACK - 1][:], ACT.Tanh)
         gated(PACK - 1, 0)
+        for t in range(PACK):
+            gated(t, 1)
 
         out_scales = keep.tile([P, H], U8, name="out_scales", align_bytes=64)
         out_words_dram = out_1[0].rearrange("p c r -> p (c r)").bitcast(I32)
-        last_chunk = len(OUT_CHUNKS) - 1
         for chunk, (c0, c1) in enumerate(OUT_CHUNKS):
-            if chunk < last_chunk:
-                for t in range(PACK):
-                    gated(t, chunk + 1)
-            width = c1 - c0
-            grouped = keep.tile([P, width, PACK], BF16, name=f"out_grouped{c0}", align_bytes=64)
-            words = keep.tile([P, width], I32, name=f"out_words{c0}", align_bytes=64)
-            if chunk < last_chunk:
-                nc.scalar.copy(*interleave_views(grouped[:], out_parts[chunk][:]))
-            else:
-                nc.vector.tensor_copy(*interleave_views(grouped[:], out_parts[chunk][:]))
-            nc.vector.quantize_mx(
-                words[:].bitcast(FP8X4), out_scales[:, c0:c1], grouped[:].rearrange("p c t -> p (c t)")
-            )
-            nc.sync.dma_start(out_words_dram[:, c0:c1], words[:])
-        for q in range(4):
+            out_grouped = keep.tile([P, c1 - c0, PACK], BF16, name=f"out_grouped{c0}", align_bytes=64)
+            out_words = keep.tile([P, c1 - c0], I32, name=f"out_words{c0}", align_bytes=64)
+            round_and_group = nc.scalar.copy if chunk == 0 else nc.vector.tensor_copy
+            round_and_group(*interleave_views(out_grouped[:], out_parts[chunk][:]))
+            quantize(nc, out_words[:], out_scales[:, c0:c1], out_grouped)
+            nc.sync.dma_start(out_words_dram[:, c0:c1], out_words[:])
+        for q in range(QUADRANTS):
             queue = nc.scalar if q % 2 else nc.sync
             queue.dma_start(out_2[0][4 * q : 4 * q + 4, :].bitcast(I32), out_scales[32 * q : 32 * q + 4, :].bitcast(I32))

from contextlib import ExitStack

import concourse.mybir as mybir

K, T, S, N, H, W = 512, 2048, 512, 512, 512, 256
FLOPS = 2 * K * S * H + 2 * S * N * H

F32 = mybir.dt.float32
BF16 = mybir.dt.bfloat16
I32 = mybir.dt.int32
U32 = mybir.dt.uint32
U16 = mybir.dt.uint16
U8 = mybir.dt.uint8
FP8X4 = mybir.dt.float8_e4m3fn_x4
ALU = mybir.AluOpType
ACT = mybir.ActivationFunctionType

P = 128
PACK = 4
QUADRANTS = 4
HALF = H // 2
PER_COL = 16

SCALE_ROWS = slice(16, 32)
OTHER_ROWS = (slice(0, 16), slice(32, 64), slice(64, P))

ROW_ORDER = (0, 2, 3, 1)

WA_LOADS = ((0, 384), (384, 512))
WA_STEPS = ((0, 0, 256), (0, 256, 384), (1, 384, 512))
Z_PIECES = ((0, 256), (256, 384), (384, 512))
Y_LATE_COLS = 64
OUT_CHUNKS = ((0, 256), (256, 512))


def spread_scale_rows(nc, plane, rows):
    for q in range(QUADRANTS):
        nc.sync.dma_start(plane[32 * q : 32 * q + 4, :].bitcast(I32), rows[4 * q : 4 * q + 4, :].bitcast(I32))


def deal_scale_bytes(nc, dealt, plain):
    nc.vector.tensor_copy(
        dealt[:].rearrange("p (t m) -> p t m", t=PACK), plain[:].rearrange("p (m t) -> p t m", t=PACK)
    )


def interleave_views(grouped, row_tiles):
    dst = grouped.rearrange("p (c i) t -> p c t i", i=4)
    src = row_tiles.rearrange("p t (c i) -> p c t i", i=4)
    return dst, src


def quantize(nc, words, scales, grouped):
    nc.vector.quantize_mx(words.bitcast(FP8X4), scales, grouped[:].rearrange("p c t -> p (c t)"))


def tile_picked_tokfillhopp_none_po_kernel(
    tc, x_words, x_scales, wa, gt, w1_words, w1_scales, offs, n1, n2, n3, n4, out_0, out_1, out_2
):
    nc = tc.nc
    with ExitStack() as ctx:
        keep = ctx.enter_context(tc.tile_pool(name="keep", bufs=1))
        y_pool = ctx.enter_context(tc.tile_pool(name="y_pool", bufs=PACK))
        psum = ctx.enter_context(tc.psum_pool(name="psum", bufs=8))

        offs_t = keep.tile([P, S // PER_COL], U16, name="offs_t")
        n1_t = keep.tile([P, W // PER_COL], U16, name="n1_t")
        n2_t = keep.tile([P, W // PER_COL], U16, name="n2_t")
        n3_t = keep.tile([P, H // PER_COL], U16, name="n3_t")
        n4_t = keep.tile([P, H // PER_COL], U16, name="n4_t")
        x_word_table = keep.tile([P, T], I32, name="x_word_table", tag="x_words", align_bytes=64)
        x_scale_table = keep.tile([P, T], U8, name="x_scale_table", align_bytes=64)
        x_scale_plane = keep.tile([P, S], U8, name="x_scale_plane", align_bytes=64)
        w1_scale_table = keep.tile([P, N], U8, name="w1_scale_table", align_bytes=64)
        gt_t = keep.tile([P, PACK], F32, name="gt_t")
        wa_raw = [
            keep.tile([P, PACK, c1 - c0], F32, name=f"wa_raw{c0}", tag=f"staged{c0}", align_bytes=64)
            for c0, c1 in WA_LOADS
        ]

        for table in (x_scale_table, w1_scale_table):
            for rows in OTHER_ROWS:
                nc.vector.memset(table[rows, :].bitcast(I32), 0)
        nc.vector.memset(x_scale_plane[:].bitcast(I32), 0)

        wa_rows = wa.rearrange("(p j) c -> p j c", j=PACK)
        nc.sync.dma_start(offs_t[:], offs)
        for table, scale_input in ((x_scale_table, x_scales), (w1_scale_table, w1_scales)):
            nc.sync.dma_start(table[SCALE_ROWS, :].bitcast(I32), scale_input[0].bitcast(I32))
        nc.sync.dma_start(wa_raw[0][:], wa_rows[:, :, WA_LOADS[0][0] : WA_LOADS[0][1]])
        for list_tile, list_input in ((n1_t, n1), (n2_t, n2), (n3_t, n3), (n4_t, n4)):
            nc.sync.dma_start(list_tile[:], list_input)
        nc.sync.dma_start(x_word_table[:], x_words[0].rearrange("p c r -> p (c r)").bitcast(I32))
        nc.sync.dma_start(wa_raw[1][:], wa_rows[:, :, WA_LOADS[1][0] : WA_LOADS[1][1]])
        nc.sync.dma_start(gt_t[:], gt.rearrange("(p t) o -> p (t o)", t=PACK))

        x_scale_picked = keep.tile([P, S], U8, name="x_scale_picked", align_bytes=64)
        x_scale_dealt = keep.tile([P, S], U8, name="x_scale_dealt", align_bytes=64)
        x_word_dealt = keep.tile([P, S], U32, name="x_word_dealt", align_bytes=64)
        nc.vector.tensor_copy(x_scale_picked[:], x_scale_table[:].indirect(offs_t[:]))
        deal_scale_bytes(nc, x_scale_dealt, x_scale_picked)
        spread_scale_rows(nc, x_scale_plane, x_scale_dealt[SCALE_ROWS, :])
        w1_scale_dealt = keep.tile([P, N], U8, name="w1_scale_dealt", align_bytes=64)
        deal_scale_bytes(nc, w1_scale_dealt, w1_scale_table)
        nc.vector.tensor_copy(
            x_word_dealt[:].rearrange("p (t m) -> p m t", t=PACK), x_word_table[:].bitcast(U32).indirect(offs_t[:])
        )

        wa_words = keep.tile([P, H], U32, name="wa_words", align_bytes=64)
        wa_scales = keep.tile([P, H], U8, name="wa_scales", align_bytes=64)
        for load, c0, c1 in WA_STEPS:
            wa_grouped = keep.tile([P, c1 - c0, PACK], BF16, name=f"wa_grouped{c0}", align_bytes=64)
            load_start = WA_LOADS[load][0]
            nc.scalar.copy(*interleave_views(wa_grouped[:], wa_raw[load][:, :, c0 - load_start : c1 - load_start]))
            quantize(nc, wa_words[:, c0:c1], wa_scales[:, c0:c1], wa_grouped)

        w1_word_raw = keep.tile([P, N], I32, name="w1_word_raw", tag="staged0", align_bytes=64)
        nc.sync.dma_start(w1_word_raw[:], w1_words[0].rearrange("p c r -> p (c r)").bitcast(I32))

        def product(lhs_words, lhs_scales, t, rhs_words, rhs_scales):
            dealt_cols = slice(t * P, (t + 1) * P)
            acc = psum.tile([P, rhs_words.shape[1]], F32, name="acc")
            nc.tensor.matmul_mx(
                acc[:],
                lhsT=lhs_words[:, dealt_cols].bitcast(FP8X4),
                lhsT_scale=lhs_scales[:, dealt_cols],
                rhs=rhs_words.bitcast(FP8X4),
                rhs_scale=rhs_scales,
                start=True,
                stop=True,
            )
            return acc

        first, second, third, last = ROW_ORDER
        y_pieces = {
            first: [(c0, c1) for load, c0, c1 in WA_STEPS],
            second: [(0, HALF), (HALF, H)],
            third: [(0, H)],
            last: [(0, H)],
        }
        y_acc = {}
        for t in ROW_ORDER:
            for c0, c1 in y_pieces[t]:
                y_acc[t, c0] = product(x_word_dealt, x_scale_plane, t, wa_words[:, c0:c1], wa_scales[:, c0:c1])

        w1_word_dealt = keep.tile([P, N], I32, name="w1_word_dealt", align_bytes=64)
        w1_scale_plane = keep.tile([P, N], U8, name="w1_scale_plane", tag="x_words", align_bytes=64)
        nc.vector.memset(w1_scale_plane[:].bitcast(I32), 0)
        spread_scale_rows(nc, w1_scale_plane, w1_scale_dealt[SCALE_ROWS, :])
        nc.vector.tensor_copy(
            w1_word_dealt[:].rearrange("p (t m) -> p m t", t=PACK), w1_word_raw[:].rearrange("p (m t) -> p m t", t=PACK)
        )

        z_grouped = [
            keep.tile([P, c1 - c0, PACK], BF16, name=f"z_grouped{c0}", align_bytes=64) for c0, c1 in Z_PIECES
        ]
        y_rows = {t: y_pool.tile([P, H], F32, name=f"y{t}", tag="y") for t in ROW_ORDER}
        for t in (first, second):
            for c0, c1 in y_pieces[t]:
                nc.scalar.copy(y_rows[t][:, c0:c1], y_acc[t, c0][:])
        early = H - Y_LATE_COLS
        nc.scalar.copy(y_rows[last][:, 0:early], y_acc[last, 0][:, 0:early])
        nc.scalar.copy(y_rows[third][:], y_acc[third, 0][:])
        nc.scalar.copy(y_rows[last][:, early:H], y_acc[last, 0][:, early:H])

        pa = {t: keep.tile([P, W], F32, name=f"pa{t}") for t in ROW_ORDER}
        pb_less_pa = {t: keep.tile([P, W], F32, name=f"pb_less_pa{t}") for t in ROW_ORDER}
        rise = {}

        def rectify(t, tile):
            rise[t] = tile
            nc.scalar.activation(rise[t][:], pb_less_pa[t][:], ACT.Relu)

        def fill(t):
            nc.vector.tensor_tensor(y_rows[t][:].indirect(n1_t[:]), pa[t][:], rise[t][:], ALU.add)

        def weigh(t):
            gate = gt_t[:, t : t + 1]
            for piece, (c0, c1) in enumerate(Z_PIECES):
                if t == last and c1 < H:
                    nc.vector.tensor_scalar(z_grouped[piece][:, :, t], y_rows[t][:, c0:c1], gate, None, ALU.mult)
                else:
                    nc.scalar.activation(z_grouped[piece][:, :, t], y_rows[t][:, c0:c1], ACT.Copy, scale=gate)

        for pair in ((first, second), (third, last)):
            for t in pair:
                nc.vector.tensor_copy(pa[t][:], y_rows[t][:].indirect(n1_t[:]))
            for t in pair:
                nc.vector.tensor_tensor(pb_less_pa[t][:], y_rows[t][:].indirect(n2_t[:]), pa[t][:], ALU.subtract)
        for t in (first, second, third):
            rectify(t, keep.tile([P, W], F32, name=f"rise{t}"))
        fill(first)
        weigh(first)
        rectify(last, y_pool.tile([P, W], F32, name="rise_last", tag="y"))
        for t in (second, third, last):
            fill(t)
            weigh(t)

        z_words = keep.tile([P, H], U32, name="z_words", align_bytes=64)
        z_scales = keep.tile([P, H], U8, name="z_scales", align_bytes=64)
        for piece, (c0, c1) in enumerate(Z_PIECES):
            quantize(nc, z_words[:, c0:c1], z_scales[:, c0:c1], z_grouped[piece])

        out_parts = [keep.tile([P, PACK, c1 - c0], F32, name=f"out_part{c0}") for c0, c1 in OUT_CHUNKS]
        out_rows = out_0.rearrange("(p t) c -> p t c", t=PACK)
        st, tanh_st = [], []

        def gated(t, chunk):
            c0, c1 = OUT_CHUNKS[chunk]
            nc.vector.tensor_tensor(
                out_parts[chunk][:, t, :],
                tanh_st[t][:].indirect(n4_t[:, c0 // PER_COL : c1 // PER_COL]),
                st[t][:, c0:c1],
                ALU.mult,
            )
            if t >= PACK - 2:
                stored = slice(0, PACK - 1) if t == PACK - 2 else slice(t, PACK)
                nc.sync.dma_start(out_rows[:, stored, c0:c1], out_parts[chunk][:, stored, :])

        for t in range(PACK):
            h_window = keep.tile([P, H], F32, name=f"h_window{t}")
            h_plain = keep.tile([P, H], F32, name=f"h_plain{t}")
            st.append(keep.tile([P, H], F32, name=f"st{t}"))
            tanh_st.append(keep.tile([P, H], F32, name=f"tanh_st{t}"))
            pieces = [slice(c0, c1) for c0, c1 in Z_PIECES] if t == 0 else [slice(0, H)]
            accs = [product(w1_word_dealt, w1_scale_plane, t, z_words[:, cols], z_scales[:, cols]) for cols in pieces]
            for cols, acc in zip(pieces, accs):
                nc.scalar.copy(h_window[:, cols], acc[:])
            for cols, acc in zip(pieces, accs):
                if cols.stop < H:
                    nc.vector.tensor_copy(h_plain[:, cols], acc[:])
                else:
                    nc.scalar.copy(h_plain[:, cols], acc[:])
            for c0 in (0, HALF):
                offsets = n3_t[:, c0 // PER_COL : (c0 + HALF) // PER_COL]
                nc.vector.tensor_tensor(
                    st[t][:, c0 : c0 + HALF], h_window[:].indirect(offsets), h_plain[:, c0 : c0 + HALF], ALU.add
                )
            if t > 0:
                nc.scalar.activation(tanh_st[t - 1][:], st[t - 1][:], ACT.Tanh)
                gated(t - 1, 0)
        nc.scalar.activation(tanh_st[PACK - 1][:], st[PACK - 1][:], ACT.Tanh)
        gated(PACK - 1, 0)
        for t in range(PACK):
            gated(t, 1)

        out_scales = keep.tile([P, H], U8, name="out_scales", align_bytes=64)
        out_words_dram = out_1[0].rearrange("p c r -> p (c r)").bitcast(I32)
        for chunk, (c0, c1) in enumerate(OUT_CHUNKS):
            out_grouped = keep.tile([P, c1 - c0, PACK], BF16, name=f"out_grouped{c0}", align_bytes=64)
            out_words = keep.tile([P, c1 - c0], I32, name=f"out_words{c0}", align_bytes=64)
            round_and_group = nc.scalar.copy if chunk == 0 else nc.vector.tensor_copy
            round_and_group(*interleave_views(out_grouped[:], out_parts[chunk][:]))
            quantize(nc, out_words[:], out_scales[:, c0:c1], out_grouped)
            nc.sync.dma_start(out_words_dram[:, c0:c1], out_words[:])
        for q in range(QUADRANTS):
            queue = nc.scalar if q % 2 else nc.sync
            queue.dma_start(out_2[0][4 * q : 4 * q + 4, :].bitcast(I32), out_scales[32 * q : 32 * q + 4, :].bitcast(I32))
